import numpy as np
import ml_dtypes


def mxq(x, axis, fmt="e4m3"):
    dtype, down = {"e4m3": (ml_dtypes.float8_e4m3fn, 7), "e5m2": (ml_dtypes.float8_e5m2, 14)}[fmt]
    v = np.moveaxis(np.asarray(x, np.float32).astype(ml_dtypes.bfloat16).astype(np.float64), axis, -1)
    blocks = v.reshape(v.shape[:-1] + (-1, 32))
    amax = np.abs(blocks).max(-1, keepdims=True)
    byte = np.maximum(np.where(amax > 0, np.frexp(amax)[1] - 1 + 127, 0) - down, 1)
    scale = np.exp2(byte - 127.0)
    codes = (blocks / scale).astype(np.float32).astype(dtype).astype(np.float64)
    return np.moveaxis((codes * scale).reshape(v.shape), -1, axis)


WIDE = False


def mx_kscale(k):
    if not WIDE:
        return np.ones(k)
    levels = np.array([30, -30])
    if k % 512:
        return np.exp2(np.random.permutation(np.resize(levels, k // 32))).repeat(32)
    a = np.empty((k // 512, 16))
    for p in range(k // 512):
        a[p, :8] = np.random.permutation(np.resize(levels, 8))
        for g in range(8):
            far = levels[np.abs(levels - a[p, g]) >= 10]
            a[p, g + 8] = far[np.random.randint(len(far))]
    return np.exp2(a.ravel()).repeat(32)


def f64(x):
    return np.asarray(x).astype(np.float64)


def striped(idx):
    return np.tile(np.asarray(idx).reshape(-1, 16).T, (8, 1)).astype(np.uint16)


def unstriped(offs):
    return offs[:16].T.reshape(-1).astype(np.int64)


E2M1 = np.array([0.0, 0.5, 1.0, 1.5, 2.0, 3.0, 4.0, 6.0, -0.0, -0.5, -1.0, -1.5, -2.0, -3.0, -4.0, -6.0])


def pack_weight(w, fmt):
    k, n = w.shape
    w = f64(np.asarray(w, np.float32).astype(ml_dtypes.bfloat16)).reshape(k // 32, 32, n)
    amax = np.abs(w).max(1)
    if fmt == "e4m3":
        byte = np.frexp(amax)[1] - 1 + 127 - 7
    else:
        mant, ex = np.frexp(amax / 6.0)
        byte = np.where(mant > 0.5, ex, ex - 1) + 127
    byte = np.clip(np.where(amax > 0, byte, 1), 1, 254)
    scaled = (w * np.exp2(127.0 - byte)[:, None, :]).reshape(k, n).astype(np.float32)
    by_word = np.ascontiguousarray(scaled.reshape(k // 512, 128, 4, n).transpose(0, 1, 3, 2))
    if fmt == "e4m3":
        words = by_word.astype(ml_dtypes.float8_e4m3fn).view(np.uint8)
    else:
        c = by_word.astype(ml_dtypes.float4_e2m1fn).view(np.uint8) & 0xF
        words = (c[..., 0::2] | (c[..., 1::2] << 4)).reshape(k // 512, 128, 2 * n)
    return np.ascontiguousarray(words), np.ascontiguousarray(byte.astype(np.uint8).reshape(k // 512, 16, n))


def unpack_weight(words, scales, fmt):
    g, _, n = scales.shape
    words = np.ascontiguousarray(words).reshape(g, 128, n, -1)
    if fmt == "e4m3":
        vals = words.view(ml_dtypes.float8_e4m3fn).astype(np.float64)
    else:
        nib = np.empty((g, 128, n, 4), np.uint8)
        nib[..., 0::2] = words & 0xF
        nib[..., 1::2] = words >> 4
        vals = E2M1[nib]
    vals = vals * np.repeat(np.exp2(scales.astype(np.float64) - 127.0), 8, axis=1)[..., None]
    return vals.transpose(0, 1, 3, 2).reshape(g * 512, n)


K, J, N, R, T, V, Q = 512, 512, 256, 256, 1024, 1024, 64


def setup_inputs():
    n = np.random.standard_normal
    idx = np.random.permutation(T)[:J]
    idx2 = np.random.permutation(V)[:J]
    fj = mx_kscale(J)
    fk = mx_kscale(K)
    drp = pack_weight(n((K, R)) * 1 / np.sqrt(K) / fk[:, None], "e2m1")
    return {
        "xf": (n((K, T))).astype(np.float32),
        "ra": (np.random.uniform(0.5, 1.5, (1, J)) * fj).astype(np.float32),
        "gt": (n((N, V)) * np.exp(0.5 * n((1, V)))).astype(np.float32),
        "rb": (np.random.uniform(0.5, 1.5, (1, J)) / fj).astype(np.float32),
        "fkr": (np.random.uniform(0.5, 1.5, (1, K)) * fk).astype(np.float32),
        "dr_words": drp[0],
        "dr_scales": drp[1],
        "gr1c": (np.random.uniform(0.5, 2.0, (R, 1))).astype(np.float32),
        "offs": striped(idx),
        "offs2": striped(idx2),
    }


def reference(xf, ra, gt, rb, fkr, dr_words, dr_scales, gr1c, offs, offs2):
    idx = unstriped(offs)
    idx2 = unstriped(offs2)
    dru = unpack_weight(dr_words, dr_scales, "e2m1")
    xg = f64(xf)[:, idx]
    x1 = np.pad(xg, ((0, 0), (1, 0)))[:, :J]
    us = (xg - 0.6 * x1) * f64(ra)
    ut = us.T
    uj = ut * f64(fkr)
    gs = f64(gt)[:, idx2] * f64(rb)
    gj = gs.T
    ujq = mxq(uj, 0, "e5m2")
    gjq = mxq(gj, 0, "e5m2")
    w = ujq.T @ gjq
    wq = mxq(w, 0, "e5m2")
    v2 = dru.T @ wq
    wq = v2.reshape(R, Q, N // Q).sum(axis=2)
    y = 0.02 * wq * f64(gr1c)
    return y

@@ -1,0 +1,190 @@
+from contextlib import ExitStack
+
+import concourse.mybir as mybir
+from concourse.masks import make_identity
+
+K, J, N, R, T, V, Q = 512, 512, 256, 256, 1024, 1024, 64
+FLOPS = 2 * J * K * N + 2 * K * R * N
+
+F32 = mybir.dt.float32
+BF16 = mybir.dt.bfloat16
+I32 = mybir.dt.int32
+U32 = mybir.dt.uint32
+U16 = mybir.dt.uint16
+U8 = mybir.dt.uint8
+E5 = mybir.dt.float8_e5m2_x4
+E2 = mybir.dt.float4_e2m1fn_x4
+MULT = mybir.AluOpType.mult
+ADD = mybir.AluOpType.add
+COPY = mybir.ActivationFunctionType.Copy
+P = 128
+PAD = 8
+QW = 4
+XMODE = "F"
+VSHARE = [256,256,0,0,0,0]
+COPY_ON_V = []
+
+
+def tile_list_directions_steps_listed_sums_kernel(tc, xf, ra, gt, rb, fkr, dr_words, dr_scales, gr1c, offs, offs2, out):
+    nc = tc.nc
+    with ExitStack() as ctx:
+        held = ctx.enter_context(tc.tile_pool(name="held", bufs=1))
+        ring = ctx.enter_context(tc.tile_pool(name="ring", bufs=2))
+        fixed = ctx.enter_context(tc.psum_pool(name="fixed", bufs=1))
+        turn = ctx.enter_context(tc.psum_pool(name="turn", bufs=4))
+
+        list_x = held.tile([P, J // 16], U16, name="list_x")
+        list_g = held.tile([P, J // 16], U16, name="list_g")
+        win = [held.tile([P, T], F32, name="win%d" % i) for i in range(6)]
+        ra_col = held.tile([P, 4], F32, name="ra_col")
+        rb_col = held.tile([P, 4], F32, name="rb_col")
+        fk_col = held.tile([P, 4], F32, name="fk_col")
+        gr_col = held.tile([P, 2], F32, name="gr_col")
+        gr_out = held.tile([P, 2], F32, name="gr_out")
+        words = held.tile([P, 2 * R], U8, name="words", align_bytes=64)
+        plane = held.tile([P, R], U8, name="plane", align_bytes=64)
+        ident = held.tile([P, P], F32, name="ident")
+
+        x_rows = xf.rearrange("(p t) v -> t p v", t=4)
+        g_rows = gt.rearrange("(m h) v -> h m v", h=2)
+        nc.sync.dma_start(list_x[:], offs)
+        nc.sync.dma_start(list_g[:], offs2)
+        nc.scalar.dma_start(fk_col[:], fkr.rearrange("o (p t) -> p (o t)", t=4))
+        nc.scalar.dma_start(ra_col[:], ra.rearrange("o (p t) -> p (o t)", t=4))
+        nc.scalar.dma_start(rb_col[:], rb.rearrange("o (p t) -> p (o t)", t=4))
+        for i in range(4):
+            nc.sync.dma_start(win[i][:], x_rows[i])
+        for h in range(2):
+            nc.sync.dma_start(win[4 + h][:], g_rows[h])
+        nc.vector.memset(plane[:].bitcast(I32), 0)
+        nc.sync.dma_start(words[:].bitcast(I32), dr_words[0].bitcast(I32))
+        for c in range(4):
+            nc.sync.dma_start(plane[32 * c : 32 * c + 4, :].bitcast(I32), dr_scales[0, 4 * c : 4 * c + 4, :].bitcast(I32))
+        with nc.allow_non_contiguous_dma(reason="one factor a partition"):
+            nc.sync.dma_start(gr_col[:], gr1c.rearrange("(h p) o -> p (h o)", h=2))
+        make_identity(nc, ident[:])
+
+        picked = [held.tile([P, PAD + J], F32, name="picked%d" % i) for i in range(6)]
+        zero = held.tile([P, 1], F32, name="zero")
+        nc.vector.memset(zero[:], 0.0)
+        for i in range(4):
+            nc.scalar.activation(picked[i][:, PAD - 1 : PAD], zero[:], COPY)
+
+        def spread(col, name):
+            bank = fixed.tile([P, 4, P], F32, name=name)
+            for t in range(4):
+                nc.tensor.transpose(bank[:, t, :], col[:, t : t + 1].to_broadcast([P, P]), ident[:])
+            return bank[:].rearrange("m t p -> m p t")
+
+        if XMODE == "B":
+            ra_all = spread(ra_col, "ra_all")
+        rb_all = spread(rb_col, "rb_all")
+
+        u_grouped = held.tile([P, 4, P, 4], BF16, name="u_grouped", align_bytes=64)
+        u_codes = held.tile([P, 4, P], U32, name="u_codes", align_bytes=64)
+        u_scales = held.tile([P, 4, P], U8, name="u_scales", align_bytes=64)
+        grouped = [u_grouped[:, i] for i in range(4)] + [held.tile([P, P, 4], BF16, name="grouped%d" % i, align_bytes=64) for i in range(4, 6)]
+        codes = [u_codes[:, i] for i in range(4)] + [held.tile([P, P], U32, name="codes%d" % i, align_bytes=64) for i in range(4, 6)]
+        scales = [u_scales[:, i] for i in range(4)] + [held.tile([P, P], U8, name="scales%d" % i, align_bytes=64) for i in range(4, 6)]
+        rounded = {}
+        diffs = {}
+        prevs = {}
+        banks = {}
+
+        def gather(i):
+            lst = list_x if i < 4 else list_g
+            nv = VSHARE[i]
+            if nv < J:
+                nc.scalar.activation(picked[i][:, PAD + nv : PAD + J], win[i][:].indirect(lst[:, nv // 16 : J // 16]), COPY)
+            if nv > 0:
+                nc.vector.tensor_copy(picked[i][:, PAD : PAD + nv], win[i][:].indirect(lst[:, 0 : nv // 16]))
+
+        def first(i):
+            now = picked[i][:, PAD : PAD + J]
+            before = picked[i][:, PAD - 1 : PAD - 1 + J]
+            if i >= 4:
+                rounded[i] = ring.tile([P, J], BF16, name="terms")
+                return
+            terms = ring.tile([P, 2, J], F32, name="terms")
+            diffs[i] = terms[:, 0, :]
+            prevs[i] = terms[:, 1, :]
+            if XMODE == "B":
+                nc.vector.scalar_tensor_tensor(diffs[i][:], before, -0.6, now, MULT, ADD)
+            else:
+                nc.vector.tensor_scalar(diffs[i][:].rearrange("p (t q) -> p q t", t=4), now.rearrange("p (q t) -> p q t", t=4), fk_col[:, i : i + 1], None, MULT)
+                nc.vector.tensor_scalar(prevs[i][:].rearrange("p (t q) -> p q t", t=4), before.rearrange("p (q t) -> p q t", t=4), fk_col[:, i : i + 1], -0.6, MULT, MULT)
+
+        def second(i):
+            if i >= 4:
+                r3 = rounded[i][:].rearrange("p (q t) -> p q t", t=4)
+                nc.vector.tensor_tensor(r3, picked[i][:, PAD : PAD + J].rearrange("p (q t) -> p q t", t=4), rb_all, MULT)
+            elif XMODE == "B":
+                nc.vector.scalar_tensor_tensor(r3, diffs[i][:].rearrange("p (q t) -> p q t", t=4), fk_col[:, i : i + 1], ra_all, MULT, MULT)
+            if i >= 4 or XMODE == "B":
+                bank = turn.tile([P, 4, P], F32, name="bank")
+                pairs = rounded[i][:].bitcast(F32)
+                for u in range(2):
+                    nc.tensor.transpose(bank[:, u, :], pairs[:, u : J // 2 : 2], ident[:])
+            else:
+                bank = turn.tile([P, 4, P], F32, name="bank")
+                for t in range(4):
+                    nc.tensor.matmul(bank[:, t, :], diffs[i][:, t * P : (t + 1) * P], ident[:], start=(t == 0), stop=False, is_transpose=True)
+                for t in range(4):
+                    nc.tensor.matmul(bank[:, t, :], prevs[i][:, t * P : (t + 1) * P], ident[:], start=False, stop=(t == 3), is_transpose=True)
+            banks[i] = bank
+
+        def third(i):
+            if i >= 4 or XMODE == "B":
+                dst = grouped[i][:].rearrange("p m t -> p (m t)").bitcast(F32).rearrange("p (m u) -> p m u", u=2)
+                src = banks[i][:, 0:2, :].rearrange("p u m -> p m u")
+                if i in COPY_ON_V:
+                    nc.vector.tensor_copy(dst, src)
+                else:
+                    nc.scalar.copy(dst, src)
+            else:
+                nc.vector.tensor_tensor(grouped[i][:], banks[i][:].rearrange("p t m -> p m t"), ra_col[:].unsqueeze(1).to_broadcast([P, P, 4]), MULT)
+
+        def fourth(i):
+            if i < 4:
+                if i % QW == QW - 1:
+                    lo = i + 1 - QW
+                    nc.vector.quantize_mx(out=u_codes[:, lo : i + 1].rearrange("p a m -> p (a m)").bitcast(E5), scales=u_scales[:, lo : i + 1].rearrange("p a m -> p (a m)"), in_=u_grouped[:, lo : i + 1].rearrange("p a m t -> p (a m t)"))
+                return
+            nc.vector.quantize_mx(out=codes[i][:].bitcast(E5), scales=scales[i][:], in_=grouped[i][:].rearrange("p m t -> p (m t)"))
+
+        w_grouped = [held.tile([P, P, 4], BF16, name="w_grouped%d" % h, align_bytes=64) for h in range(2)]
+        w_codes = [held.tile([P, P], U32, name="w_codes%d" % h, align_bytes=64) for h in range(2)]
+        w_scales = [held.tile([P, P], U8, name="w_scales%d" % h, align_bytes=64) for h in range(2)]
+        v_bank = [fixed.tile([P, P], F32, name="v_bank%d" % s) for s in range(2)]
+
+        def moment(h):
+            w_bank = turn.tile([P, 4, P], F32, name="bank")
+            for t in range(4):
+                nc.tensor.matmul_mx(out=w_bank[:, t, :], lhsT=codes[t][:].bitcast(E5), lhsT_scale=scales[t][:], rhs=codes[4 + h][:].bitcast(E5), rhs_scale=scales[4 + h][:], start=True, stop=True)
+            nc.scalar.copy(w_grouped[h][:], w_bank[:].rearrange("p t m -> p m t"))
+            nc.vector.quantize_mx(out=w_codes[h][:].bitcast(E5), scales=w_scales[h][:], in_=w_grouped[h][:].rearrange("p m t -> p (m t)"))
+            for s in range(2):
+                nc.tensor.matmul_mx(out=v_bank[s][:], lhsT=words[:, 2 * P * s : 2 * P * (s + 1)].bitcast(E2), lhsT_scale=plane[:, P * s : P * (s + 1)], rhs=w_codes[h][:].bitcast(E5), rhs_scale=w_scales[h][:], start=(h == 0), stop=(h == 1))
+
+        for step in range(8):
+            if step < 6:
+                gather(step)
+            if 0 <= step - 2 < 6:
+                third(step - 2)
+            if step < 6:
+                first(step)
+                second(step)
+            if 0 <= step - 2 < 6:
+                fourth(step - 2)
+            if step == 2:
+                nc.vector.tensor_scalar(gr_out[:], gr_col[:], 0.02, None, MULT)
+            if step >= 6:
+                moment(step - 6)
+
+        odd = held.tile([P, 2, Q], F32, name="odd")
+        res = held.tile([P, 2, Q], F32, name="res")
+        for s in range(2):
+            nc.vector.tensor_scalar(odd[:, s, :], v_bank[s][:, 1:P:2], gr_out[:, s : s + 1], None, MULT)
+        for s in range(2):
+            nc.vector.scalar_tensor_tensor(res[:, s, :], v_bank[s][:, 0:P:2], gr_out[:, s : s + 1], odd[:, s, :], MULT, ADD)
+        nc.sync.dma_start(out.rearrange("(s p) q -> p s q", s=2), res[:])

@@ -19,23 +19,26 @@ ADD = mybir.AluOpType.add
 COPY = mybir.ActivationFunctionType.Copy
 P = 128
 PAD = 8
-QW = 4
-XMODE = "F"
-VSHARE = [256,256,0,0,0,0]
+VSHARE = [256,0,0,0,0,0]
+PARTS = 1
+AFTER = [4,5]
 COPY_ON_V = []
+W_ON_V = []
 
 
 def tile_list_directions_steps_listed_sums_kernel(tc, xf, ra, gt, rb, fkr, dr_words, dr_scales, gr1c, offs, offs2, out):
     nc = tc.nc
     with ExitStack() as ctx:
         held = ctx.enter_context(tc.tile_pool(name="held", bufs=1))
-        ring = ctx.enter_context(tc.tile_pool(name="ring", bufs=2))
+        ring = ctx.enter_context(tc.tile_pool(name="ring", bufs=4))
+        late = ctx.enter_context(tc.tile_pool(name="late", bufs=1))
         fixed = ctx.enter_context(tc.psum_pool(name="fixed", bufs=1))
-        turn = ctx.enter_context(tc.psum_pool(name="turn", bufs=4))
 
         list_x = held.tile([P, J // 16], U16, name="list_x")
         list_g = held.tile([P, J // 16], U16, name="list_g")
-        win = [held.tile([P, T], F32, name="win%d" % i) for i in range(6)]
+        win = [held.tile([P, T], F32, name="win%d" % i, tag="win%d" % i, align_bytes=64) for i in range(5)]
+        last = late.tile([P, 5 * J // 2], F32, name="last", offset=0, align_bytes=64)
+        win.append(last[:, 0:T])
         ra_col = held.tile([P, 4], F32, name="ra_col")
         rb_col = held.tile([P, 4], F32, name="rb_col")
         fk_col = held.tile([P, 4], F32, name="fk_col")
@@ -47,12 +50,14 @@ def tile_list_directions_steps_listed_sums_kernel(tc, xf, ra, gt, rb, fkr, dr_wo
 
         x_rows = xf.rearrange("(p t) v -> t p v", t=4)
         g_rows = gt.rearrange("(m h) v -> h m v", h=2)
+        nc.sync.dma_start(win[0][:], x_rows[0])
         nc.sync.dma_start(list_x[:], offs)
+        nc.sync.dma_start(ra_col[:], ra.rearrange("o (p t) -> p (o t)", t=4))
+        nc.sync.dma_start(fk_col[:], fkr.rearrange("o (p t) -> p (o t)", t=4))
+        nc.sync.dma_start(win[1][:], x_rows[1])
         nc.sync.dma_start(list_g[:], offs2)
-        nc.scalar.dma_start(fk_col[:], fkr.rearrange("o (p t) -> p (o t)", t=4))
-        nc.scalar.dma_start(ra_col[:], ra.rearrange("o (p t) -> p (o t)", t=4))
-        nc.scalar.dma_start(rb_col[:], rb.rearrange("o (p t) -> p (o t)", t=4))
-        for i in range(4):
+        nc.sync.dma_start(rb_col[:], rb.rearrange("o (p t) -> p (o t)", t=4))
+        for i in range(2, 4):
             nc.sync.dma_start(win[i][:], x_rows[i])
         for h in range(2):
             nc.sync.dma_start(win[4 + h][:], g_rows[h])
@@ -76,81 +81,60 @@ def tile_list_directions_steps_listed_sums_kernel(tc, xf, ra, gt, rb, fkr, dr_wo
                 nc.tensor.transpose(bank[:, t, :], col[:, t : t + 1].to_broadcast([P, P]), ident[:])
             return bank[:].rearrange("m t p -> m p t")
 
-        if XMODE == "B":
-            ra_all = spread(ra_col, "ra_all")
+        ra_all = spread(ra_col, "ra_all")
         rb_all = spread(rb_col, "rb_all")
 
-        u_grouped = held.tile([P, 4, P, 4], BF16, name="u_grouped", align_bytes=64)
         u_codes = held.tile([P, 4, P], U32, name="u_codes", align_bytes=64)
         u_scales = held.tile([P, 4, P], U8, name="u_scales", align_bytes=64)
-        grouped = [u_grouped[:, i] for i in range(4)] + [held.tile([P, P, 4], BF16, name="grouped%d" % i, align_bytes=64) for i in range(4, 6)]
         codes = [u_codes[:, i] for i in range(4)] + [held.tile([P, P], U32, name="codes%d" % i, align_bytes=64) for i in range(4, 6)]
         scales = [u_scales[:, i] for i in range(4)] + [held.tile([P, P], U8, name="scales%d" % i, align_bytes=64) for i in range(4, 6)]
-        rounded = {}
-        diffs = {}
-        prevs = {}
+        rounded = [held.tile([P, J], BF16, name="rounded%d" % i) for i in range(6)]
         banks = {}
 
         def gather(i):
             lst = list_x if i < 4 else list_g
             nv = VSHARE[i]
-            if nv < J:
-                nc.scalar.activation(picked[i][:, PAD + nv : PAD + J], win[i][:].indirect(lst[:, nv // 16 : J // 16]), COPY)
+            nc.scalar.activation(picked[i][:, PAD + nv : PAD + J], win[i][:].indirect(lst[:, nv // 16 : J // 16]), COPY)
             if nv > 0:
                 nc.vector.tensor_copy(picked[i][:, PAD : PAD + nv], win[i][:].indirect(lst[:, 0 : nv // 16]))
 
-        def first(i):
-            now = picked[i][:, PAD : PAD + J]
-            before = picked[i][:, PAD - 1 : PAD - 1 + J]
-            if i >= 4:
-                rounded[i] = ring.tile([P, J], BF16, name="terms")
-                return
-            terms = ring.tile([P, 2, J], F32, name="terms")
-            diffs[i] = terms[:, 0, :]
-            prevs[i] = terms[:, 1, :]
-            if XMODE == "B":
-                nc.vector.scalar_tensor_tensor(diffs[i][:], before, -0.6, now, MULT, ADD)
-            else:
-                nc.vector.tensor_scalar(diffs[i][:].rearrange("p (t q) -> p q t", t=4), now.rearrange("p (q t) -> p q t", t=4), fk_col[:, i : i + 1], None, MULT)
-                nc.vector.tensor_scalar(prevs[i][:].rearrange("p (t q) -> p q t", t=4), before.rearrange("p (q t) -> p q t", t=4), fk_col[:, i : i + 1], -0.6, MULT, MULT)
-
-        def second(i):
-            if i >= 4:
-                r3 = rounded[i][:].rearrange("p (q t) -> p q t", t=4)
-                nc.vector.tensor_tensor(r3, picked[i][:, PAD : PAD + J].rearrange("p (q t) -> p q t", t=4), rb_all, MULT)
-            elif XMODE == "B":
-                nc.vector.scalar_tensor_tensor(r3, diffs[i][:].rearrange("p (q t) -> p q t", t=4), fk_col[:, i : i + 1], ra_all, MULT, MULT)
-            if i >= 4 or XMODE == "B":
-                bank = turn.tile([P, 4, P], F32, name="bank")
-                pairs = rounded[i][:].bitcast(F32)
-                for u in range(2):
-                    nc.tensor.transpose(bank[:, u, :], pairs[:, u : J // 2 : 2], ident[:])
-            else:
-                bank = turn.tile([P, 4, P], F32, name="bank")
-                for t in range(4):
-                    nc.tensor.matmul(bank[:, t, :], diffs[i][:, t * P : (t + 1) * P], ident[:], start=(t == 0), stop=False, is_transpose=True)
-                for t in range(4):
-                    nc.tensor.matmul(bank[:, t, :], prevs[i][:, t * P : (t + 1) * P], ident[:], start=False, stop=(t == 3), is_transpose=True)
-            banks[i] = bank
-
-        def third(i):
-            if i >= 4 or XMODE == "B":
-                dst = grouped[i][:].rearrange("p m t -> p (m t)").bitcast(F32).rearrange("p (m u) -> p m u", u=2)
-                src = banks[i][:, 0:2, :].rearrange("p u m -> p m u")
-                if i in COPY_ON_V:
-                    nc.vector.tensor_copy(dst, src)
-                else:
-                    nc.scalar.copy(dst, src)
-            else:
-                nc.vector.tensor_tensor(grouped[i][:], banks[i][:].rearrange("p t m -> p m t"), ra_col[:].unsqueeze(1).to_broadcast([P, P, 4]), MULT)
-
-        def fourth(i):
+        def weigh(i):
+            w = J // PARTS
             if i < 4:
-                if i % QW == QW - 1:
-                    lo = i + 1 - QW
-                    nc.vector.quantize_mx(out=u_codes[:, lo : i + 1].rearrange("p a m -> p (a m)").bitcast(E5), scales=u_scales[:, lo : i + 1].rearrange("p a m -> p (a m)"), in_=u_grouped[:, lo : i + 1].rearrange("p a m t -> p (a m t)"))
-                return
-            nc.vector.quantize_mx(out=codes[i][:].bitcast(E5), scales=scales[i][:], in_=grouped[i][:].rearrange("p m t -> p (m t)"))
+                diffs = [ring.tile([P, w], F32, name="diffs") for a in range(PARTS)]
+                for a in range(PARTS):
+                    nc.vector.scalar_tensor_tensor(diffs[a][:], picked[i][:, PAD - 1 + a * w : PAD - 1 + (a + 1) * w], -0.6, picked[i][:, PAD + a * w : PAD + (a + 1) * w], MULT, ADD)
+                for a in range(PARTS):
+                    nc.vector.scalar_tensor_tensor(rounded[i][:, a * w : (a + 1) * w].rearrange("p (q t) -> p q t", t=4), diffs[a][:].rearrange("p (q t) -> p q t", t=4), fk_col[:, i : i + 1], ra_all[:, a * w // 4 : (a + 1) * w // 4, :], MULT, MULT)
+            else:
+                for a, b in ((VSHARE[i], J), (0, VSHARE[i])):
+                    if b > a:
+                        nc.vector.tensor_tensor(rounded[i][:, a:b].rearrange("p (q t) -> p q t", t=4), picked[i][:, PAD + a : PAD + b].rearrange("p (q t) -> p q t", t=4), rb_all[:, a // 4 : b // 4, :], MULT)
+            if i >= 4 or i % 2 == 0:
+                banks[i] = fixed.tile([P, 4, P], F32, name="turn%d" % i, tag="turn%d" % i)
+                lo = 0
+            else:
+                banks[i] = banks[i - 1]
+                lo = 2
+            pairs = rounded[i][:].bitcast(F32)
+            for u in range(2):
+                nc.tensor.transpose(banks[i][:, lo + u, :], pairs[:, u : J // 2 : 2], ident[:])
+
+        def copy_words(on_v, dst, src):
+            if on_v:
+                nc.vector.tensor_copy(dst, src)
+            else:
+                nc.scalar.copy(dst, src)
+
+        def quantise_u(a):
+            grouped = late.tile([P, 2 * J], BF16, name="u_grouped%d" % a, offset=4 * J * a, align_bytes=64)
+            copy_words(a in COPY_ON_V, grouped[:].bitcast(F32).rearrange("p (i m u) -> p i m u", i=2, u=2), banks[2 * a][:].rearrange("p (i u) m -> p i m u", u=2))
+            nc.vector.quantize_mx(out=u_codes[:, 2 * a : 2 * a + 2].rearrange("p a m -> p (a m)").bitcast(E5), scales=u_scales[:, 2 * a : 2 * a + 2].rearrange("p a m -> p (a m)"), in_=grouped[:])
+
+        def quantise_g(i):
+            grouped = late.tile([P, J], BF16, name="g_grouped%d" % i, offset=2 * J * i, align_bytes=64)
+            copy_words(i in COPY_ON_V, grouped[:].bitcast(F32).rearrange("p (m u) -> p m u", u=2), banks[i][:, 0:2, :].rearrange("p u m -> p m u"))
+            nc.vector.quantize_mx(out=codes[i][:].bitcast(E5), scales=scales[i][:], in_=grouped[:])
 
         w_grouped = [held.tile([P, P, 4], BF16, name="w_grouped%d" % h, align_bytes=64) for h in range(2)]
         w_codes = [held.tile([P, P], U32, name="w_codes%d" % h, align_bytes=64) for h in range(2)]
@@ -158,28 +142,28 @@ def tile_list_directions_steps_listed_sums_kernel(tc, xf, ra, gt, rb, fkr, dr_wo
         v_bank = [fixed.tile([P, P], F32, name="v_bank%d" % s) for s in range(2)]
 
         def moment(h):
-            w_bank = turn.tile([P, 4, P], F32, name="bank")
+            w_bank = fixed.tile([P, 4, P], F32, name="w_bank%d" % h, tag="turn%d" % (2 * h))
             for t in range(4):
                 nc.tensor.matmul_mx(out=w_bank[:, t, :], lhsT=codes[t][:].bitcast(E5), lhsT_scale=scales[t][:], rhs=codes[4 + h][:].bitcast(E5), rhs_scale=scales[4 + h][:], start=True, stop=True)
-            nc.scalar.copy(w_grouped[h][:], w_bank[:].rearrange("p t m -> p m t"))
+            copy_words(h in W_ON_V, w_grouped[h][:], w_bank[:].rearrange("p t m -> p m t"))
             nc.vector.quantize_mx(out=w_codes[h][:].bitcast(E5), scales=w_scales[h][:], in_=w_grouped[h][:].rearrange("p m t -> p (m t)"))
+
+        def directions(h):
             for s in range(2):
                 nc.tensor.matmul_mx(out=v_bank[s][:], lhsT=words[:, 2 * P * s : 2 * P * (s + 1)].bitcast(E2), lhsT_scale=plane[:, P * s : P * (s + 1)], rhs=w_codes[h][:].bitcast(E5), rhs_scale=w_scales[h][:], start=(h == 0), stop=(h == 1))
 
-        for step in range(8):
-            if step < 6:
-                gather(step)
-            if 0 <= step - 2 < 6:
-                third(step - 2)
-            if step < 6:
-                first(step)
-                second(step)
-            if 0 <= step - 2 < 6:
-                fourth(step - 2)
-            if step == 2:
-                nc.vector.tensor_scalar(gr_out[:], gr_col[:], 0.02, None, MULT)
-            if step >= 6:
-                moment(step - 6)
+        for i in range(6):
+            gather(i)
+            weigh(i)
+        nc.vector.tensor_scalar(gr_out[:], gr_col[:], 0.02, None, MULT)
+        quantise_u(0)
+        quantise_u(1)
+        quantise_g(4)
+        quantise_g(5)
+        moment(0)
+        moment(1)
+        directions(0)
+        directions(1)
 
         odd = held.tile([P, 2, Q], F32, name="odd")
         res = held.tile([P, 2, Q], F32, name="res")

@@ -37,8 +37,8 @@ def tile_list_directions_steps_listed_sums_kernel(tc, xf, ra, gt, rb, fkr, dr_wo
         list_x = held.tile([P, J // 16], U16, name="list_x")
         list_g = held.tile([P, J // 16], U16, name="list_g")
         win = [held.tile([P, T], F32, name="win%d" % i, tag="win%d" % i, align_bytes=64) for i in range(5)]
-        last = late.tile([P, 5 * J // 2], F32, name="last", offset=0, align_bytes=64)
-        win.append(last[:, 0:T])
+        last = late.tile([P, T], F32, name="last", offset=0, align_bytes=64)
+        win.append(last)
         ra_col = held.tile([P, 4], F32, name="ra_col")
         rb_col = held.tile([P, 4], F32, name="rb_col")
         fk_col = held.tile([P, 4], F32, name="fk_col")
@@ -76,7 +76,7 @@ def tile_list_directions_steps_listed_sums_kernel(tc, xf, ra, gt, rb, fkr, dr_wo
             nc.scalar.activation(picked[i][:, PAD - 1 : PAD], zero[:], COPY)
 
         def spread(col, name):
-            bank = fixed.tile([P, 4, P], F32, name=name)
+            bank = fixed.tile([P, 4, P], F32, name=name, tag=name)
             for t in range(4):
                 nc.tensor.transpose(bank[:, t, :], col[:, t : t + 1].to_broadcast([P, P]), ident[:])
             return bank[:].rearrange("m t p -> m p t")
@@ -84,11 +84,8 @@ def tile_list_directions_steps_listed_sums_kernel(tc, xf, ra, gt, rb, fkr, dr_wo
         ra_all = spread(ra_col, "ra_all")
         rb_all = spread(rb_col, "rb_all")
 
-        u_codes = held.tile([P, 4, P], U32, name="u_codes", align_bytes=64)
-        u_scales = held.tile([P, 4, P], U8, name="u_scales", align_bytes=64)
-        codes = [u_codes[:, i] for i in range(4)] + [held.tile([P, P], U32, name="codes%d" % i, align_bytes=64) for i in range(4, 6)]
-        scales = [u_scales[:, i] for i in range(4)] + [held.tile([P, P], U8, name="scales%d" % i, align_bytes=64) for i in range(4, 6)]
-        rounded = [held.tile([P, J], BF16, name="rounded%d" % i) for i in range(6)]
+        codes = {}
+        scales = {}
         banks = {}
 
         def gather(i):
@@ -99,26 +96,21 @@ def tile_list_directions_steps_listed_sums_kernel(tc, xf, ra, gt, rb, fkr, dr_wo
                 nc.vector.tensor_copy(picked[i][:, PAD : PAD + nv], win[i][:].indirect(lst[:, 0 : nv // 16]))
 
         def weigh(i):
-            w = J // PARTS
+            now = picked[i][:, PAD : PAD + J]
             if i < 4:
-                diffs = [ring.tile([P, w], F32, name="diffs") for a in range(PARTS)]
-                for a in range(PARTS):
-                    nc.vector.scalar_tensor_tensor(diffs[a][:], picked[i][:, PAD - 1 + a * w : PAD - 1 + (a + 1) * w], -0.6, picked[i][:, PAD + a * w : PAD + (a + 1) * w], MULT, ADD)
-                for a in range(PARTS):
-                    nc.vector.scalar_tensor_tensor(rounded[i][:, a * w : (a + 1) * w].rearrange("p (q t) -> p q t", t=4), diffs[a][:].rearrange("p (q t) -> p q t", t=4), fk_col[:, i : i + 1], ra_all[:, a * w // 4 : (a + 1) * w // 4, :], MULT, MULT)
-            else:
-                for a, b in ((VSHARE[i], J), (0, VSHARE[i])):
-                    if b > a:
-                        nc.vector.tensor_tensor(rounded[i][:, a:b].rearrange("p (q t) -> p q t", t=4), picked[i][:, PAD + a : PAD + b].rearrange("p (q t) -> p q t", t=4), rb_all[:, a // 4 : b // 4, :], MULT)
-            if i >= 4 or i % 2 == 0:
-                banks[i] = fixed.tile([P, 4, P], F32, name="turn%d" % i, tag="turn%d" % i)
-                lo = 0
-            else:
-                banks[i] = banks[i - 1]
-                lo = 2
-            pairs = rounded[i][:].bitcast(F32)
+                diff = ring.tile([P, J], F32, name="diff")
+                nc.vector.scalar_tensor_tensor(diff[:], picked[i][:, PAD - 1 : PAD - 1 + J], -0.6, now, MULT, ADD)
+                now = diff[:]
+            banks[i] = fixed.tile([P, 4, P], F32, name="turn%d" % i, tag="turn%d" % i)
+            lo = 0
             for u in range(2):
-                nc.tensor.transpose(banks[i][:, lo + u, :], pairs[:, u : J // 2 : 2], ident[:])
+                src = now.rearrange("p (q t) -> p q t", t=4)[:, :, 2 * u : 2 * u + 2]
+                half = held.tile([P, P, 2], BF16, name="half%d_%d" % (i, u))
+                if i < 4:
+                    nc.vector.scalar_tensor_tensor(half[:], src, fk_col[:, i : i + 1], ra_all[:, :, 2 * u : 2 * u + 2], MULT, MULT)
+                else:
+                    nc.vector.tensor_tensor(half[:], src, rb_all[:, :, 2 * u : 2 * u + 2], MULT)
+                nc.tensor.transpose(banks[i][:, lo + u, :], half[:].rearrange("p q e -> p (q e)").bitcast(F32), ident[:])
 
         def copy_words(on_v, dst, src):
             if on_v:
@@ -126,23 +118,36 @@ def tile_list_directions_steps_listed_sums_kernel(tc, xf, ra, gt, rb, fkr, dr_wo
             else:
                 nc.scalar.copy(dst, src)
 
-        def quantise_u(a):
-            grouped = late.tile([P, 2 * J], BF16, name="u_grouped%d" % a, offset=4 * J * a, align_bytes=64)
-            copy_words(a in COPY_ON_V, grouped[:].bitcast(F32).rearrange("p (i m u) -> p i m u", i=2, u=2), banks[2 * a][:].rearrange("p (i u) m -> p i m u", u=2))
-            nc.vector.quantize_mx(out=u_codes[:, 2 * a : 2 * a + 2].rearrange("p a m -> p (a m)").bitcast(E5), scales=u_scales[:, 2 * a : 2 * a + 2].rearrange("p a m -> p (a m)"), in_=grouped[:])
+        def leave_bank(on_v, dst, i):
+            copy_words(on_v, dst.bitcast(F32).rearrange("p (m u) -> p m u", u=2), banks[i][:, 0:2, :].rearrange("p u m -> p m u"))
 
-        def quantise_g(i):
-            grouped = late.tile([P, J], BF16, name="g_grouped%d" % i, offset=2 * J * i, align_bytes=64)
-            copy_words(i in COPY_ON_V, grouped[:].bitcast(F32).rearrange("p (m u) -> p m u", u=2), banks[i][:, 0:2, :].rearrange("p u m -> p m u"))
+        def quantise_one(i, grouped, words_tile, on_v):
+            codes[i] = words_tile
+            scales[i] = held.tile([P, P], U8, name="scales%d" % i, align_bytes=64)
+            leave_bank(on_v, grouped[:], i)
             nc.vector.quantize_mx(out=codes[i][:].bitcast(E5), scales=scales[i][:], in_=grouped[:])
+
+        def quantise_all():
+            quantise_one(0, held.tile([P, J], BF16, name="grouped0", tag="win1", align_bytes=64), held.tile([P, P], U32, name="codes0", tag="win3", align_bytes=64), True)
+            quantise_one(1, held.tile([P, J], BF16, name="grouped1", tag="win2", align_bytes=64), late.tile([P, P], U32, name="codes1", offset=3072, align_bytes=64), True)
+            both = late.tile([P, 2 * J], BF16, name="grouped23", offset=0, align_bytes=64)
+            both_codes = held.tile([P, 2 * P], U32, name="codes23", align_bytes=64)
+            both_scales = held.tile([P, 2 * P], U8, name="scales23", align_bytes=64)
+            for a in range(2):
+                leave_bank(False, both[:, a * J : (a + 1) * J], 2 + a)
+                codes[2 + a] = both_codes[:, a * P : (a + 1) * P]
+                scales[2 + a] = both_scales[:, a * P : (a + 1) * P]
+            nc.vector.quantize_mx(out=both_codes[:].bitcast(E5), scales=both_scales[:], in_=both[:])
+            quantise_one(4, late.tile([P, J], BF16, name="grouped4", offset=2048, align_bytes=64), held.tile([P, P], U32, name="codes4", align_bytes=64), False)
+            quantise_one(5, held.tile([P, J], BF16, name="grouped5", align_bytes=64), held.tile([P, P], U32, name="codes5", align_bytes=64), False)
 
         w_grouped = [held.tile([P, P, 4], BF16, name="w_grouped%d" % h, align_bytes=64) for h in range(2)]
         w_codes = [held.tile([P, P], U32, name="w_codes%d" % h, align_bytes=64) for h in range(2)]
         w_scales = [held.tile([P, P], U8, name="w_scales%d" % h, align_bytes=64) for h in range(2)]
-        v_bank = [fixed.tile([P, P], F32, name="v_bank%d" % s) for s in range(2)]
+        v_bank = [fixed.tile([P, P], F32, name="v_bank%d" % s, tag=("ra_all", "rb_all")[s]) for s in range(2)]
 
         def moment(h):
-            w_bank = fixed.tile([P, 4, P], F32, name="w_bank%d" % h, tag="turn%d" % (2 * h))
+            w_bank = fixed.tile([P, 4, P], F32, name="w_bank%d" % h, tag="turn%d" % h)
             for t in range(4):
                 nc.tensor.matmul_mx(out=w_bank[:, t, :], lhsT=codes[t][:].bitcast(E5), lhsT_scale=scales[t][:], rhs=codes[4 + h][:].bitcast(E5), rhs_scale=scales[4 + h][:], start=True, stop=True)
             copy_words(h in W_ON_V, w_grouped[h][:], w_bank[:].rearrange("p t m -> p m t"))
@@ -156,10 +161,7 @@ def tile_list_directions_steps_listed_sums_kernel(tc, xf, ra, gt, rb, fkr, dr_wo
             gather(i)
             weigh(i)
         nc.vector.tensor_scalar(gr_out[:], gr_col[:], 0.02, None, MULT)
-        quantise_u(0)
-        quantise_u(1)
-        quantise_g(4)
-        quantise_g(5)
+        quantise_all()
         moment(0)
         moment(1)
         directions(0)

from contextlib import ExitStack

import concourse.mybir as mybir
from concourse.masks import make_identity

K, J, N, R, T, V, Q = 512, 512, 256, 256, 1024, 1024, 64
FLOPS = 2 * J * K * N + 2 * K * R * N

F32 = mybir.dt.float32
BF16 = mybir.dt.bfloat16
I32 = mybir.dt.int32
U32 = mybir.dt.uint32
U16 = mybir.dt.uint16
U8 = mybir.dt.uint8
E5 = mybir.dt.float8_e5m2_x4
E2 = mybir.dt.float4_e2m1fn_x4
MULT = mybir.AluOpType.mult
ADD = mybir.AluOpType.add
COPY = mybir.ActivationFunctionType.Copy
P = 128
PAD = 8
VSHARE = [256,0,0,0,0,0]
PARTS = 1
AFTER = [4,5]
COPY_ON_V = []
W_ON_V = []


def tile_list_directions_steps_listed_sums_kernel(tc, xf, ra, gt, rb, fkr, dr_words, dr_scales, gr1c, offs, offs2, out):
    nc = tc.nc
    with ExitStack() as ctx:
        held = ctx.enter_context(tc.tile_pool(name="held", bufs=1))
        ring = ctx.enter_context(tc.tile_pool(name="ring", bufs=4))
        late = ctx.enter_context(tc.tile_pool(name="late", bufs=1))
        fixed = ctx.enter_context(tc.psum_pool(name="fixed", bufs=1))

        list_x = held.tile([P, J // 16], U16, name="list_x")
        list_g = held.tile([P, J // 16], U16, name="list_g")
        win = [held.tile([P, T], F32, name="win%d" % i, tag="win%d" % i, align_bytes=64) for i in range(5)]
        last = late.tile([P, T], F32, name="last", offset=0, align_bytes=64)
        win.append(last)
        ra_col = held.tile([P, 4], F32, name="ra_col")
        rb_col = held.tile([P, 4], F32, name="rb_col")
        fk_col = held.tile([P, 4], F32, name="fk_col")
        gr_col = held.tile([P, 2], F32, name="gr_col")
        gr_out = held.tile([P, 2], F32, name="gr_out")
        words = held.tile([P, 2 * R], U8, name="words", align_bytes=64)
        plane = held.tile([P, R], U8, name="plane", align_bytes=64)
        ident = held.tile([P, P], F32, name="ident")

        x_rows = xf.rearrange("(p t) v -> t p v", t=4)
        g_rows = gt.rearrange("(m h) v -> h m v", h=2)
        nc.sync.dma_start(win[0][:], x_rows[0])
        nc.sync.dma_start(list_x[:], offs)
        nc.sync.dma_start(ra_col[:], ra.rearrange("o (p t) -> p (o t)", t=4))
        nc.sync.dma_start(fk_col[:], fkr.rearrange("o (p t) -> p (o t)", t=4))
        nc.sync.dma_start(win[1][:], x_rows[1])
        nc.sync.dma_start(list_g[:], offs2)
        nc.sync.dma_start(rb_col[:], rb.rearrange("o (p t) -> p (o t)", t=4))
        for i in range(2, 4):
            nc.sync.dma_start(win[i][:], x_rows[i])
        for h in range(2):
            nc.sync.dma_start(win[4 + h][:], g_rows[h])
        nc.vector.memset(plane[:].bitcast(I32), 0)
        nc.sync.dma_start(words[:].bitcast(I32), dr_words[0].bitcast(I32))
        for c in range(4):
            nc.sync.dma_start(plane[32 * c : 32 * c + 4, :].bitcast(I32), dr_scales[0, 4 * c : 4 * c + 4, :].bitcast(I32))
        with nc.allow_non_contiguous_dma(reason="one factor a partition"):
            nc.sync.dma_start(gr_col[:], gr1c.rearrange("(h p) o -> p (h o)", h=2))
        make_identity(nc, ident[:])

        picked = [held.tile([P, PAD + J], F32, name="picked%d" % i) for i in range(6)]
        zero = held.tile([P, 1], F32, name="zero")
        nc.vector.memset(zero[:], 0.0)
        for i in range(4):
            nc.scalar.activation(picked[i][:, PAD - 1 : PAD], zero[:], COPY)

        def spread(col, name):
            bank = fixed.tile([P, 4, P], F32, name=name, tag=name)
            for t in range(4):
                nc.tensor.transpose(bank[:, t, :], col[:, t : t + 1].to_broadcast([P, P]), ident[:])
            return bank[:].rearrange("m t p -> m p t")

        ra_all = spread(ra_col, "ra_all")
        rb_all = spread(rb_col, "rb_all")

        codes = {}
        scales = {}
        banks = {}

        def gather(i):
            lst = list_x if i < 4 else list_g
            nv = VSHARE[i]
            nc.scalar.activation(picked[i][:, PAD + nv : PAD + J], win[i][:].indirect(lst[:, nv // 16 : J // 16]), COPY)
            if nv > 0:
                nc.vector.tensor_copy(picked[i][:, PAD : PAD + nv], win[i][:].indirect(lst[:, 0 : nv // 16]))

        def weigh(i):
            now = picked[i][:, PAD : PAD + J]
            if i < 4:
                diff = ring.tile([P, J], F32, name="diff")
                nc.vector.scalar_tensor_tensor(diff[:], picked[i][:, PAD - 1 : PAD - 1 + J], -0.6, now, MULT, ADD)
                now = diff[:]
            banks[i] = fixed.tile([P, 4, P], F32, name="turn%d" % i, tag="turn%d" % i)
            lo = 0
            for u in range(2):
                src = now.rearrange("p (q t) -> p q t", t=4)[:, :, 2 * u : 2 * u + 2]
                half = held.tile([P, P, 2], BF16, name="half%d_%d" % (i, u))
                if i < 4:
                    nc.vector.scalar_tensor_tensor(half[:], src, fk_col[:, i : i + 1], ra_all[:, :, 2 * u : 2 * u + 2], MULT, MULT)
                else:
                    nc.vector.tensor_tensor(half[:], src, rb_all[:, :, 2 * u : 2 * u + 2], MULT)
                nc.tensor.transpose(banks[i][:, lo + u, :], half[:].rearrange("p q e -> p (q e)").bitcast(F32), ident[:])

        def copy_words(on_v, dst, src):
            if on_v:
                nc.vector.tensor_copy(dst, src)
            else:
                nc.scalar.copy(dst, src)

        def leave_bank(on_v, dst, i):
            copy_words(on_v, dst.bitcast(F32).rearrange("p (m u) -> p m u", u=2), banks[i][:, 0:2, :].rearrange("p u m -> p m u"))

        def quantise_one(i, grouped, words_tile, on_v):
            codes[i] = words_tile
            scales[i] = held.tile([P, P], U8, name="scales%d" % i, align_bytes=64)
            leave_bank(on_v, grouped[:], i)
            nc.vector.quantize_mx(out=codes[i][:].bitcast(E5), scales=scales[i][:], in_=grouped[:])

        def quantise_all():
            quantise_one(0, held.tile([P, J], BF16, name="grouped0", tag="win1", align_bytes=64), held.tile([P, P], U32, name="codes0", tag="win3", align_bytes=64), True)
            quantise_one(1, held.tile([P, J], BF16, name="grouped1", tag="win2", align_bytes=64), late.tile([P, P], U32, name="codes1", offset=3072, align_bytes=64), True)
            both = late.tile([P, 2 * J], BF16, name="grouped23", offset=0, align_bytes=64)
            both_codes = held.tile([P, 2 * P], U32, name="codes23", align_bytes=64)
            both_scales = held.tile([P, 2 * P], U8, name="scales23", align_bytes=64)
            for a in range(2):
                leave_bank(False, both[:, a * J : (a + 1) * J], 2 + a)
                codes[2 + a] = both_codes[:, a * P : (a + 1) * P]
                scales[2 + a] = both_scales[:, a * P : (a + 1) * P]
            nc.vector.quantize_mx(out=both_codes[:].bitcast(E5), scales=both_scales[:], in_=both[:])
            quantise_one(4, late.tile([P, J], BF16, name="grouped4", offset=2048, align_bytes=64), held.tile([P, P], U32, name="codes4", align_bytes=64), False)
            quantise_one(5, held.tile([P, J], BF16, name="grouped5", align_bytes=64), held.tile([P, P], U32, name="codes5", align_bytes=64), False)

        w_grouped = [held.tile([P, P, 4], BF16, name="w_grouped%d" % h, align_bytes=64) for h in range(2)]
        w_codes = [held.tile([P, P], U32, name="w_codes%d" % h, align_bytes=64) for h in range(2)]
        w_scales = [held.tile([P, P], U8, name="w_scales%d" % h, align_bytes=64) for h in range(2)]
        v_bank = [fixed.tile([P, P], F32, name="v_bank%d" % s, tag=("ra_all", "rb_all")[s]) for s in range(2)]

        def moment(h):
            w_bank = fixed.tile([P, 4, P], F32, name="w_bank%d" % h, tag="turn%d" % h)
            for t in range(4):
                nc.tensor.matmul_mx(out=w_bank[:, t, :], lhsT=codes[t][:].bitcast(E5), lhsT_scale=scales[t][:], rhs=codes[4 + h][:].bitcast(E5), rhs_scale=scales[4 + h][:], start=True, stop=True)
            copy_words(h in W_ON_V, w_grouped[h][:], w_bank[:].rearrange("p t m -> p m t"))
            nc.vector.quantize_mx(out=w_codes[h][:].bitcast(E5), scales=w_scales[h][:], in_=w_grouped[h][:].rearrange("p m t -> p (m t)"))

        def directions(h):
            for s in range(2):
                nc.tensor.matmul_mx(out=v_bank[s][:], lhsT=words[:, 2 * P * s : 2 * P * (s + 1)].bitcast(E2), lhsT_scale=plane[:, P * s : P * (s + 1)], rhs=w_codes[h][:].bitcast(E5), rhs_scale=w_scales[h][:], start=(h == 0), stop=(h == 1))

        for i in range(6):
            gather(i)
            weigh(i)
        nc.vector.tensor_scalar(gr_out[:], gr_col[:], 0.02, None, MULT)
        quantise_all()
        moment(0)
        moment(1)
        directions(0)
        directions(1)

        odd = held.tile([P, 2, Q], F32, name="odd")
        res = held.tile([P, 2, Q], F32, name="res")
        for s in range(2):
            nc.vector.tensor_scalar(odd[:, s, :], v_bank[s][:, 1:P:2], gr_out[:, s : s + 1], None, MULT)
        for s in range(2):
            nc.vector.scalar_tensor_tensor(res[:, s, :], v_bank[s][:, 0:P:2], gr_out[:, s : s + 1], odd[:, s, :], MULT, ADD)
        nc.sync.dma_start(out.rearrange("(s p) q -> p s q", s=2), res[:])
